import numpy as np, ml_dtypes
CORES = [36,164,52,180,100,228,116,244]
N = 8
TK = 512
def gelu(z): return 0.5 * z * (1.0 + np.tanh(0.7978845608028654 * (z + 0.044715 * z ** 3)))
def setup_inputs(rng):
    return {"x": rng.standard_normal((N, 128, TK), dtype=np.float32).astype(ml_dtypes.bfloat16), "w1": (rng.standard_normal((N, 128, 128), dtype=np.float32) / 8).astype(ml_dtypes.bfloat16), "w2": (rng.standard_normal((N, 128, 128), dtype=np.float32) / 8).astype(ml_dtypes.bfloat16)}
def setup_inputs_big(rng):
    d = setup_inputs(rng)
    for k in ("x",): d[k] = (d[k].astype(np.float32) * 1024.0).astype(d[k].dtype)
    return d
def setup_inputs_small(rng):
    d = setup_inputs(rng)
    for k in ("x",): d[k] = (d[k].astype(np.float32) * (1 / 1024.0)).astype(d[k].dtype)
    return d
def setup_inputs_apart(rng):
    d = setup_inputs(rng)
    f = (10.0 ** rng.permutation(np.linspace(-1.5, 1.5, N))).astype(np.float32).reshape(N, 1, 1)
    for k in ("x",): d[k] = (d[k].astype(np.float32) * f).astype(d[k].dtype)
    return d
def reference(x, w1, w2):
    X, W1, W2 = x.astype(np.float64), w1.astype(np.float64), w2.astype(np.float64)
    y = np.zeros((N, 128, TK))
    for r in range(N):
        for j in range(N):
            y[r] += W2[j].T @ (gelu(W1[j].T @ X[r]))
    return {"y": y.astype(ml_dtypes.bfloat16)}

@@ -1,0 +1,121 @@
+from concourse.mybir import ActivationFunctionType
+
+D = 128
+WW = 2 * D
+TK = 512
+HALF = TK // 2
+QUART = TK // 4
+NB = 4
+NR = 8
+
+SCRATCH = {
+    "wall": ("sbuf", [128, NR * WW], "bfloat16"),
+    "xs": ("sbuf", [128, TK], "bfloat16"),
+    "hs": ("sbuf", [128, NB * HALF], "bfloat16"),
+    "ys": ("sbuf", [128, TK], "bfloat16"),
+}
+for _k in range(NB):
+    SCRATCH["hp%d" % _k] = ("psum", [128, 512], "float32")
+    SCRATCH["yp%d" % _k] = ("psum", [128, 512], "float32")
+
+SEMAPHORES = (["ldw", "ldx", "sent", "st", "cp0", "cp1"]
+              + ["arr%d" % j for j in range(NR)]
+              + ["m1_%d" % k for k in range(NB)]
+              + ["ga_%d" % k for k in range(NB)]
+              + ["m2_%d" % k for k in range(NB)]
+              + ["yd%d" % q for q in range(4)])
+
+
+def _bits(m):
+    return bin(m).count("1")
+
+
+def rank_program(g, core, T, topo):
+    r = T.rank_of(core)
+    if r is None:
+        return
+    n = len(T.cores)
+    tot, seen = {}, {}
+
+    def inc(ins, name, k):
+        ins.then_inc(T.sem[name], k)
+        tot[name] = tot.get(name, 0) + k
+
+    def wait(q, name, v):
+        q.wait_ge(T.sem[name], v)
+        seen[name] = max(seen.get(name, 0), v)
+
+    def slot(j):
+        return T.wall[:, j * WW:(j + 1) * WW]
+
+    def w1(j):
+        return T.wall[:, j * WW:j * WW + D]
+
+    def w2(j):
+        return T.wall[:, j * WW + D:(j + 1) * WW]
+
+    inc(g.sync.dma_start(w1(r), T.w1[:, :]), "ldw", 16)
+    inc(g.scalar.dma_start(w2(r), T.w2[:, :]), "ldw", 16)
+    inc(g.sync.dma_start(T.xs[:, :], T.x[:, :]), "ldx", 16)
+
+    wait(g, "ldw", 32)
+    for k in range(1, n):
+        d = T.cores[(r + k) % n]
+        rid, pid = topo.addr(d, core)
+        m = topo.mask(core, d)
+        g.remote_dma(out_ap=slot(r), in_ap=slot(r), remote_sem=T.sem["arr%d" % r], local_sem=T.sem.sent,
+                     pid=pid, routing_id=rid, dma_engine_mask=m)
+        tot["sent"] = tot.get("sent", 0) + _bits(m)
+    for j in range(n):
+        if j != r:
+            tot["arr%d" % j] = _bits(topo.mask(T.cores[j], core))
+
+    pe = g.tensor
+    order = [(r - p) % n for p in range(n)]
+    wait(pe, "ldw", 32)
+    wait(pe, "ldx", 16)
+    for p, j in enumerate(order):
+        if p > 0:
+            wait(pe, "arr%d" % j, tot["arr%d" % j])
+        for h in range(2):
+            i = 2 * p + h
+            k, u = i % NB, i // NB
+            if u > 0:
+                wait(pe, "ga_%d" % k, u)
+            inc(pe.matmul(T["hp%d" % k][:, 0:HALF], w1(j), T.xs[:, h * HALF:(h + 1) * HALF], True, True),
+                "m1_%d" % k, 1)
+        for h in range(2):
+            i = 2 * p + h
+            k, u = i % NB, i // NB
+            wait(pe, "ga_%d" % k, u + 1)
+            for s in range(2):
+                q = 2 * h + s
+                ins = pe.matmul(T["yp%d" % q][:, 0:QUART], w2(j),
+                                T.hs[:, k * HALF + s * QUART:k * HALF + (s + 1) * QUART], p == 0, p == n - 1)
+                inc(ins, ("yd%d" % q) if p == n - 1 else ("m2_%d" % k), 1)
+
+    act = g.scalar
+    for i in range(2 * n):
+        k, u = i % NB, i // NB
+        wait(act, "m1_%d" % k, u + 1)
+        if u > 0:
+            wait(act, "m2_%d" % k, 2 * u)
+        inc(act.activation(T.hs[:, k * HALF:(k + 1) * HALF], T["hp%d" % k][:, 0:HALF],
+                           ActivationFunctionType.Gelu_apprx_tanh), "ga_%d" % k, 1)
+
+    for q in range(4):
+        dst, src = T.ys[:, q * QUART:(q + 1) * QUART], T["yp%d" % q][:, 0:QUART]
+        if q % 2 == 0:
+            wait(g.vector, "yd%d" % q, 1)
+            inc(g.vector.tensor_copy(dst, src), "cp%d" % (q // 2), 1)
+        else:
+            wait(act, "yd%d" % q, 1)
+            inc(act.activation(dst, src, ActivationFunctionType.Copy), "cp%d" % (q // 2), 1)
+    for h in range(2):
+        wait(g.sync, "cp%d" % h, 2)
+        inc(g.sync.dma_start(T.y[:, h * HALF:(h + 1) * HALF], T.ys[:, h * HALF:(h + 1) * HALF]), "st", 16)
+    wait(g.sync, "st", 32)
+
+    for name in sorted(tot):
+        if seen.get(name, 0) < tot[name]:
+            wait(g, name, tot[name])

@@ -1,4 +1,4 @@
-from concourse.mybir import ActivationFunctionType
+from concourse.mybir import ActivationFunctionType, AluOpType
 
 D = 128
 WW = 2 * D
@@ -7,18 +7,22 @@ HALF = TK // 2
 QUART = TK // 4
 NB = 4
 NR = 8
+NCORES = 256
+HB = (1, 2)
+SEND = ("x", 1, 3, 2, 4, 5, 6, 7)
 
 SCRATCH = {
     "wall": ("sbuf", [128, NR * WW], "bfloat16"),
     "xs": ("sbuf", [128, TK], "bfloat16"),
     "hs": ("sbuf", [128, NB * HALF], "bfloat16"),
     "ys": ("sbuf", [128, TK], "bfloat16"),
+    "part": ("sbuf", [128, TK], "bfloat16"),
 }
 for _k in range(NB):
     SCRATCH["hp%d" % _k] = ("psum", [128, 512], "float32")
     SCRATCH["yp%d" % _k] = ("psum", [128, 512], "float32")
 
-SEMAPHORES = (["ldw", "ldx", "sent", "st", "cp0", "cp1"]
+SEMAPHORES = (["ldw", "ldx", "sent", "st", "cp0", "cp1", "xarr", "par0", "par1"]
               + ["arr%d" % j for j in range(NR)]
               + ["m1_%d" % k for k in range(NB)]
               + ["ga_%d" % k for k in range(NB)]
@@ -30,11 +34,23 @@ def _bits(m):
     return bin(m).count("1")
 
 
+def _helper(topo, c):
+    for h in range(NCORES):
+        if h != c and topo.host(h) == topo.host(c) and topo.chip(h) == topo.chip(c) and topo.die(h) == topo.die(c):
+            return h
+    return None
+
+
 def rank_program(g, core, T, topo):
-    r = T.rank_of(core)
-    if r is None:
-        return
     n = len(T.cores)
+    r = T.rank_of(core)
+    is_rank = r is not None
+    helpers = [_helper(topo, c) for c in T.cores]
+    if not is_rank:
+        if core not in helpers:
+            return
+        r = helpers.index(core)
+    rcore, hcore = T.cores[r], helpers[r]
     tot, seen = {}, {}
 
     def inc(ins, name, k):
@@ -45,6 +61,16 @@ def rank_program(g, core, T, topo):
         q.wait_ge(T.sem[name], v)
         seen[name] = max(seen.get(name, 0), v)
 
+    def eng(src, dst):
+        return topo.mask(src, dst) & topo.mask(src, T.cores[(r + 1) % n])
+
+    def send(dst, out_ap, in_ap, sem):
+        rid, pid = topo.addr(dst, core)
+        m = eng(core, dst)
+        g.remote_dma(out_ap=out_ap, in_ap=in_ap, remote_sem=T.sem[sem], local_sem=T.sem.sent,
+                     pid=pid, routing_id=rid, dma_engine_mask=m)
+        tot["sent"] = tot.get("sent", 0) + _bits(m)
+
     def slot(j):
         return T.wall[:, j * WW:(j + 1) * WW]
 
@@ -54,36 +80,47 @@ def rank_program(g, core, T, topo):
     def w2(j):
         return T.wall[:, j * WW + D:(j + 1) * WW]
 
-    inc(g.sync.dma_start(w1(r), T.w1[:, :]), "ldw", 16)
-    inc(g.scalar.dma_start(w2(r), T.w2[:, :]), "ldw", 16)
-    inc(g.sync.dma_start(T.xs[:, :], T.x[:, :]), "ldx", 16)
+    def half(t, h):
+        return t[:, h * HALF:(h + 1) * HALF]
 
-    wait(g, "ldw", 32)
-    for k in range(1, n):
-        d = T.cores[(r + k) % n]
-        rid, pid = topo.addr(d, core)
-        m = topo.mask(core, d)
-        g.remote_dma(out_ap=slot(r), in_ap=slot(r), remote_sem=T.sem["arr%d" % r], local_sem=T.sem.sent,
-                     pid=pid, routing_id=rid, dma_engine_mask=m)
-        tot["sent"] = tot.get("sent", 0) + _bits(m)
-    for j in range(n):
+    nbits = _bits(eng(rcore, hcore))
+    pe, act = g.tensor, g.scalar
+
+    if is_rank:
+        inc(g.sync.dma_start(T.xs[:, :], T.x[:, :]), "ldx", 16)
+        inc(g.scalar.dma_start(w1(r), T.w1[:, :]), "ldw", 16)
+        inc(g.sync.dma_start(w2(r), T.w2[:, :]), "ldw", 16)
+        for it in SEND:
+            if it == "x":
+                wait(g, "ldx", 16)
+                send(hcore, T.xs[:, :], T.xs[:, :], "xarr")
+            else:
+                wait(g, "ldw", 32)
+                dr = (r + it) % n
+                send(helpers[dr] if it in HB else T.cores[dr], slot(r), slot(r), "arr%d" % r)
+        order = [r] + [(r - k) % n for k in SEND if k != "x" and k not in HB]
+        for h in range(2):
+            tot["par%d" % h] = nbits
+        wait(pe, "ldw", 32)
+        wait(pe, "ldx", 16)
+    else:
+        order = [(r - k) % n for k in SEND if k in HB]
+        tot["xarr"] = nbits
+        wait(pe, "xarr", nbits)
+    for j in order:
         if j != r:
-            tot["arr%d" % j] = _bits(topo.mask(T.cores[j], core))
+            tot["arr%d" % j] = nbits
+    nblk = len(order)
 
-    pe = g.tensor
-    order = [(r - p) % n for p in range(n)]
-    wait(pe, "ldw", 32)
-    wait(pe, "ldx", 16)
     for p, j in enumerate(order):
-        if p > 0:
-            wait(pe, "arr%d" % j, tot["arr%d" % j])
+        if j != r:
+            wait(pe, "arr%d" % j, nbits)
         for h in range(2):
             i = 2 * p + h
             k, u = i % NB, i // NB
             if u > 0:
                 wait(pe, "ga_%d" % k, u)
-            inc(pe.matmul(T["hp%d" % k][:, 0:HALF], w1(j), T.xs[:, h * HALF:(h + 1) * HALF], True, True),
-                "m1_%d" % k, 1)
+            inc(pe.matmul(T["hp%d" % k][:, 0:HALF], w1(j), half(T.xs, h), True, True), "m1_%d" % k, 1)
         for h in range(2):
             i = 2 * p + h
             k, u = i % NB, i // NB
@@ -91,11 +128,10 @@ def rank_program(g, core, T, topo):
             for s in range(2):
                 q = 2 * h + s
                 ins = pe.matmul(T["yp%d" % q][:, 0:QUART], w2(j),
-                                T.hs[:, k * HALF + s * QUART:k * HALF + (s + 1) * QUART], p == 0, p == n - 1)
-                inc(ins, ("yd%d" % q) if p == n - 1 else ("m2_%d" % k), 1)
+                                T.hs[:, k * HALF + s * QUART:k * HALF + (s + 1) * QUART], p == 0, p == nblk - 1)
+                inc(ins, ("yd%d" % q) if p == nblk - 1 else ("m2_%d" % k), 1)
 
-    act = g.scalar
-    for i in range(2 * n):
+    for i in range(2 * nblk):
         k, u = i % NB, i // NB
         wait(act, "m1_%d" % k, u + 1)
         if u > 0:
@@ -105,16 +141,26 @@ def rank_program(g, core, T, topo):
 
     for q in range(4):
         dst, src = T.ys[:, q * QUART:(q + 1) * QUART], T["yp%d" % q][:, 0:QUART]
-        if q % 2 == 0:
+        if is_rank:
+            wait(g.vector, "par%d" % (q // 2), nbits)
+            wait(g.vector, "yd%d" % q, 1)
+            inc(g.vector.tensor_tensor(dst, src, T.part[:, q * QUART:(q + 1) * QUART], AluOpType.add),
+                "cp%d" % (q // 2), 1)
+        elif q % 2 == 0:
             wait(g.vector, "yd%d" % q, 1)
             inc(g.vector.tensor_copy(dst, src), "cp%d" % (q // 2), 1)
         else:
             wait(act, "yd%d" % q, 1)
             inc(act.activation(dst, src, ActivationFunctionType.Copy), "cp%d" % (q // 2), 1)
     for h in range(2):
-        wait(g.sync, "cp%d" % h, 2)
-        inc(g.sync.dma_start(T.y[:, h * HALF:(h + 1) * HALF], T.ys[:, h * HALF:(h + 1) * HALF]), "st", 16)
-    wait(g.sync, "st", 32)
+        if is_rank:
+            wait(g.sync, "cp%d" % h, 2)
+            inc(g.sync.dma_start(half(T.y, h), half(T.ys, h)), "st", 16)
+        else:
+            wait(g, "cp%d" % h, 2)
+            send(rcore, half(T.part, h), half(T.ys, h), "par%d" % h)
+    if is_rank:
+        wait(g.sync, "st", 32)
 
     for name in sorted(tot):
         if seen.get(name, 0) < tot[name]:

@@ -6,15 +6,17 @@ TK = 512
 HALF = TK // 2
 QUART = TK // 4
 NB = 4
+NP = 6
 NR = 8
 NCORES = 256
-HB = (1, 2)
-SEND = ("x", 1, 3, 2, 4, 5, 6, 7)
+HB = (1, 2, 3)
+SEND = (1, "x0", 4, "x1", 2, 3, 5, 6, 7)
+PIECES = ((0, 2), (2, 3), (3, 4))
 
 SCRATCH = {
     "wall": ("sbuf", [128, NR * WW], "bfloat16"),
     "xs": ("sbuf", [128, TK], "bfloat16"),
-    "hs": ("sbuf", [128, NB * HALF], "bfloat16"),
+    "hs": ("sbuf", [128, NP * HALF], "bfloat16"),
     "ys": ("sbuf", [128, TK], "bfloat16"),
     "part": ("sbuf", [128, TK], "bfloat16"),
 }
@@ -22,12 +24,13 @@ for _k in range(NB):
     SCRATCH["hp%d" % _k] = ("psum", [128, 512], "float32")
     SCRATCH["yp%d" % _k] = ("psum", [128, 512], "float32")
 
-SEMAPHORES = (["ldw", "ldx", "sent", "st", "cp0", "cp1", "xarr", "par0", "par1"]
+SEMAPHORES = (["ldw", "ldx", "sent", "st", "x0", "x1", "par0", "par1", "par2"]
               + ["arr%d" % j for j in range(NR)]
-              + ["m1_%d" % k for k in range(NB)]
-              + ["ga_%d" % k for k in range(NB)]
+              + ["m1_%d" % k for k in range(NP)]
+              + ["ga_%d" % k for k in range(NP)]
               + ["m2_%d" % k for k in range(NB)]
-              + ["yd%d" % q for q in range(4)])
+              + ["yd%d" % q for q in range(4)]
+              + ["cq%d" % q for q in range(4)])
 
 
 def _bits(m):
@@ -52,6 +55,7 @@ def rank_program(g, core, T, topo):
         r = helpers.index(core)
     rcore, hcore = T.cores[r], helpers[r]
     tot, seen = {}, {}
+    gelu = ActivationFunctionType.Gelu_apprx_tanh
 
     def inc(ins, name, k):
         ins.then_inc(T.sem[name], k)
@@ -61,12 +65,11 @@ def rank_program(g, core, T, topo):
         q.wait_ge(T.sem[name], v)
         seen[name] = max(seen.get(name, 0), v)
 
-    def eng(src, dst):
-        return topo.mask(src, dst) & topo.mask(src, T.cores[(r + 1) % n])
+    def far(src):
+        return topo.mask(src, T.cores[(r + 1) % n])
 
-    def send(dst, out_ap, in_ap, sem):
+    def send(dst, out_ap, in_ap, sem, m):
         rid, pid = topo.addr(dst, core)
-        m = eng(core, dst)
         g.remote_dma(out_ap=out_ap, in_ap=in_ap, remote_sem=T.sem[sem], local_sem=T.sem.sent,
                      pid=pid, routing_id=rid, dma_engine_mask=m)
         tot["sent"] = tot.get("sent", 0) + _bits(m)
@@ -83,38 +86,91 @@ def rank_program(g, core, T, topo):
     def half(t, h):
         return t[:, h * HALF:(h + 1) * HALF]
 
-    nbits = _bits(eng(rcore, hcore))
+    def quarts(t, a, b):
+        return t[:, a * QUART:b * QUART]
+
+    def finish():
+        for name in sorted(tot):
+            if seen.get(name, 0) < tot[name]:
+                wait(g, name, tot[name])
+
+    wbits = _bits(far(rcore))
+    xmask = topo.mask(rcore, hcore) & ~far(rcore)
+    xbits = _bits(xmask)
+    pmask = topo.mask(hcore, rcore) & far(hcore)
+    pbits = _bits(pmask)
     pe, act = g.tensor, g.scalar
 
-    if is_rank:
-        inc(g.sync.dma_start(T.xs[:, :], T.x[:, :]), "ldx", 16)
-        inc(g.scalar.dma_start(w1(r), T.w1[:, :]), "ldw", 16)
-        inc(g.sync.dma_start(w2(r), T.w2[:, :]), "ldw", 16)
-        for it in SEND:
-            if it == "x":
-                wait(g, "ldx", 16)
-                send(hcore, T.xs[:, :], T.xs[:, :], "xarr")
-            else:
-                wait(g, "ldw", 32)
-                dr = (r + it) % n
-                send(helpers[dr] if it in HB else T.cores[dr], slot(r), slot(r), "arr%d" % r)
-        order = [r] + [(r - k) % n for k in SEND if k != "x" and k not in HB]
+    if not is_rank:
+        blocks = [(r - k) % n for k in SEND if k in HB]
+        nb = len(blocks)
+        tot["x0"], tot["x1"] = xbits, xbits
+        for j in blocks:
+            tot["arr%d" % j] = wbits
+
+        def hview(h, i):
+            return T["hp%d" % h][:, 0:HALF] if i == 0 else half(T["hp%d" % (i + 1)], h)
+
+        for i in range(nb):
+            wait(pe, "arr%d" % blocks[i], wbits)
+            for h in range(2):
+                wait(pe, "x%d" % h, xbits)
+                inc(pe.matmul(hview(h, i), w1(blocks[i]), half(T.xs, h), True, True), "m1_%d" % (h * nb + i), 1)
         for h in range(2):
-            tot["par%d" % h] = nbits
-        wait(pe, "ldw", 32)
-        wait(pe, "ldx", 16)
-    else:
-        order = [(r - k) % n for k in SEND if k in HB]
-        tot["xarr"] = nbits
-        wait(pe, "xarr", nbits)
+            for i in range(nb):
+                c = h * nb + i
+                wait(pe, "ga_%d" % c, 1)
+                for s in range(2):
+                    q = 2 * h + s
+                    ins = pe.matmul(T["yp%d" % q][:, 0:QUART], w2(blocks[i]),
+                                    T.hs[:, c * HALF + s * QUART:c * HALF + (s + 1) * QUART], i == 0, i == nb - 1)
+                    inc(ins, ("yd%d" % q) if i == nb - 1 else "m2_0", 1)
+        for h in range(2):
+            for i in range(nb):
+                wait(act, "m1_%d" % (h * nb + i), 1)
+                if i > 0:
+                    wait(act, "m1_%d" % ((1 - h) * nb + i), 1)
+                inc(act.activation(half(T.hs, h * nb + i), hview(h, i), gelu), "ga_%d" % (h * nb + i), 1)
+        for q in range(4):
+            dst, src = quarts(T.ys, q, q + 1), T["yp%d" % q][:, 0:QUART]
+            if q < 3:
+                wait(g.vector, "yd%d" % q, 1)
+                inc(g.vector.tensor_copy(dst, src), "cq%d" % q, 1)
+            else:
+                wait(act, "yd%d" % q, 1)
+                inc(act.activation(dst, src, ActivationFunctionType.Copy), "cq%d" % q, 1)
+        for k, (a, b) in enumerate(PIECES):
+            for q in range(a, b):
+                wait(g, "cq%d" % q, 1)
+            send(rcore, quarts(T.part, a, b), quarts(T.ys, a, b), "par%d" % k, pmask)
+        finish()
+        return
+
+    inc(g.sync.dma_start(w1(r), T.w1[:, :]), "ldw", 16)
+    inc(g.scalar.dma_start(w2(r), T.w2[:, :]), "ldw", 16)
+    inc(g.sync.dma_start(T.xs[:, :], T.x[:, :]), "ldx", 16)
+    for it in SEND:
+        if it in ("x0", "x1"):
+            h = 0 if it == "x0" else 1
+            wait(g, "ldx", 16)
+            send(hcore, half(T.xs, h), half(T.xs, h), it, xmask)
+        else:
+            wait(g, "ldw", 32)
+            dr = (r + it) % n
+            send(helpers[dr] if it in HB else T.cores[dr], slot(r), slot(r), "arr%d" % r, far(core))
+    order = [r] + [(r - k) % n for k in SEND if k not in ("x0", "x1") and k not in HB]
+    for k in range(len(PIECES)):
+        tot["par%d" % k] = pbits
     for j in order:
         if j != r:
-            tot["arr%d" % j] = nbits
+            tot["arr%d" % j] = wbits
     nblk = len(order)
 
+    wait(pe, "ldw", 32)
+    wait(pe, "ldx", 16)
     for p, j in enumerate(order):
         if j != r:
-            wait(pe, "arr%d" % j, nbits)
+            wait(pe, "arr%d" % j, wbits)
         for h in range(2):
             i = 2 * p + h
             k, u = i % NB, i // NB
@@ -136,32 +192,15 @@ def rank_program(g, core, T, topo):
         wait(act, "m1_%d" % k, u + 1)
         if u > 0:
             wait(act, "m2_%d" % k, 2 * u)
-        inc(act.activation(T.hs[:, k * HALF:(k + 1) * HALF], T["hp%d" % k][:, 0:HALF],
-                           ActivationFunctionType.Gelu_apprx_tanh), "ga_%d" % k, 1)
+        inc(act.activation(half(T.hs, k), T["hp%d" % k][:, 0:HALF], gelu), "ga_%d" % k, 1)
 
-    for q in range(4):
-        dst, src = T.ys[:, q * QUART:(q + 1) * QUART], T["yp%d" % q][:, 0:QUART]
-        if is_rank:
-            wait(g.vector, "par%d" % (q // 2), nbits)
+    for k, (a, b) in enumerate(PIECES):
+        wait(g.vector, "par%d" % k, pbits)
+        for q in range(a, b):
             wait(g.vector, "yd%d" % q, 1)
-            inc(g.vector.tensor_tensor(dst, src, T.part[:, q * QUART:(q + 1) * QUART], AluOpType.add),
-                "cp%d" % (q // 2), 1)
-        elif q % 2 == 0:
-            wait(g.vector, "yd%d" % q, 1)
-            inc(g.vector.tensor_copy(dst, src), "cp%d" % (q // 2), 1)
-        else:
-            wait(act, "yd%d" % q, 1)
-            inc(act.activation(dst, src, ActivationFunctionType.Copy), "cp%d" % (q // 2), 1)
-    for h in range(2):
-        if is_rank:
-            wait(g.sync, "cp%d" % h, 2)
-            inc(g.sync.dma_start(half(T.y, h), half(T.ys, h)), "st", 16)
-        else:
-            wait(g, "cp%d" % h, 2)
-            send(rcore, half(T.part, h), half(T.ys, h), "par%d" % h)
-    if is_rank:
-        wait(g.sync, "st", 32)
-
-    for name in sorted(tot):
-        if seen.get(name, 0) < tot[name]:
-            wait(g, name, tot[name])
+            inc(g.vector.tensor_tensor(quarts(T.ys, q, q + 1), T["yp%d" % q][:, 0:QUART],
+                                       quarts(T.part, q, q + 1), AluOpType.add), "cq%d" % q, 1)
+            wait(g.sync, "cq%d" % q, 1)
+        inc(g.sync.dma_start(quarts(T.y, a, b), quarts(T.ys, a, b)), "st", 16)
+    wait(g.sync, "st", 16 * len(PIECES))
+    finish()

from concourse.mybir import ActivationFunctionType, AluOpType

D = 128
WW = 2 * D
TK = 512
HALF = TK // 2
QUART = TK // 4
NB = 4
NP = 6
NR = 8
NCORES = 256
HB = (1, 2, 3)
SEND = (1, "x0", 4, "x1", 2, 3, 5, 6, 7)
PIECES = ((0, 2), (2, 3), (3, 4))

SCRATCH = {
    "wall": ("sbuf", [128, NR * WW], "bfloat16"),
    "xs": ("sbuf", [128, TK], "bfloat16"),
    "hs": ("sbuf", [128, NP * HALF], "bfloat16"),
    "ys": ("sbuf", [128, TK], "bfloat16"),
    "part": ("sbuf", [128, TK], "bfloat16"),
}
for _k in range(NB):
    SCRATCH["hp%d" % _k] = ("psum", [128, 512], "float32")
    SCRATCH["yp%d" % _k] = ("psum", [128, 512], "float32")

SEMAPHORES = (["ldw", "ldx", "sent", "st", "x0", "x1", "par0", "par1", "par2"]
              + ["arr%d" % j for j in range(NR)]
              + ["m1_%d" % k for k in range(NP)]
              + ["ga_%d" % k for k in range(NP)]
              + ["m2_%d" % k for k in range(NB)]
              + ["yd%d" % q for q in range(4)]
              + ["cq%d" % q for q in range(4)])


def _bits(m):
    return bin(m).count("1")


def _helper(topo, c):
    for h in range(NCORES):
        if h != c and topo.host(h) == topo.host(c) and topo.chip(h) == topo.chip(c) and topo.die(h) == topo.die(c):
            return h
    return None


def rank_program(g, core, T, topo):
    n = len(T.cores)
    r = T.rank_of(core)
    is_rank = r is not None
    helpers = [_helper(topo, c) for c in T.cores]
    if not is_rank:
        if core not in helpers:
            return
        r = helpers.index(core)
    rcore, hcore = T.cores[r], helpers[r]
    tot, seen = {}, {}
    gelu = ActivationFunctionType.Gelu_apprx_tanh

    def inc(ins, name, k):
        ins.then_inc(T.sem[name], k)
        tot[name] = tot.get(name, 0) + k

    def wait(q, name, v):
        q.wait_ge(T.sem[name], v)
        seen[name] = max(seen.get(name, 0), v)

    def far(src):
        return topo.mask(src, T.cores[(r + 1) % n])

    def send(dst, out_ap, in_ap, sem, m):
        rid, pid = topo.addr(dst, core)
        g.remote_dma(out_ap=out_ap, in_ap=in_ap, remote_sem=T.sem[sem], local_sem=T.sem.sent,
                     pid=pid, routing_id=rid, dma_engine_mask=m)
        tot["sent"] = tot.get("sent", 0) + _bits(m)

    def slot(j):
        return T.wall[:, j * WW:(j + 1) * WW]

    def w1(j):
        return T.wall[:, j * WW:j * WW + D]

    def w2(j):
        return T.wall[:, j * WW + D:(j + 1) * WW]

    def half(t, h):
        return t[:, h * HALF:(h + 1) * HALF]

    def quarts(t, a, b):
        return t[:, a * QUART:b * QUART]

    def finish():
        for name in sorted(tot):
            if seen.get(name, 0) < tot[name]:
                wait(g, name, tot[name])

    wbits = _bits(far(rcore))
    xmask = topo.mask(rcore, hcore) & ~far(rcore)
    xbits = _bits(xmask)
    pmask = topo.mask(hcore, rcore) & far(hcore)
    pbits = _bits(pmask)
    pe, act = g.tensor, g.scalar

    if not is_rank:
        blocks = [(r - k) % n for k in SEND if k in HB]
        nb = len(blocks)
        tot["x0"], tot["x1"] = xbits, xbits
        for j in blocks:
            tot["arr%d" % j] = wbits

        def hview(h, i):
            return T["hp%d" % h][:, 0:HALF] if i == 0 else half(T["hp%d" % (i + 1)], h)

        for i in range(nb):
            wait(pe, "arr%d" % blocks[i], wbits)
            for h in range(2):
                wait(pe, "x%d" % h, xbits)
                inc(pe.matmul(hview(h, i), w1(blocks[i]), half(T.xs, h), True, True), "m1_%d" % (h * nb + i), 1)
        for h in range(2):
            for i in range(nb):
                c = h * nb + i
                wait(pe, "ga_%d" % c, 1)
                for s in range(2):
                    q = 2 * h + s
                    ins = pe.matmul(T["yp%d" % q][:, 0:QUART], w2(blocks[i]),
                                    T.hs[:, c * HALF + s * QUART:c * HALF + (s + 1) * QUART], i == 0, i == nb - 1)
                    inc(ins, ("yd%d" % q) if i == nb - 1 else "m2_0", 1)
        for h in range(2):
            for i in range(nb):
                wait(act, "m1_%d" % (h * nb + i), 1)
                if i > 0:
                    wait(act, "m1_%d" % ((1 - h) * nb + i), 1)
                inc(act.activation(half(T.hs, h * nb + i), hview(h, i), gelu), "ga_%d" % (h * nb + i), 1)
        for q in range(4):
            dst, src = quarts(T.ys, q, q + 1), T["yp%d" % q][:, 0:QUART]
            if q < 3:
                wait(g.vector, "yd%d" % q, 1)
                inc(g.vector.tensor_copy(dst, src), "cq%d" % q, 1)
            else:
                wait(act, "yd%d" % q, 1)
                inc(act.activation(dst, src, ActivationFunctionType.Copy), "cq%d" % q, 1)
        for k, (a, b) in enumerate(PIECES):
            for q in range(a, b):
                wait(g, "cq%d" % q, 1)
            send(rcore, quarts(T.part, a, b), quarts(T.ys, a, b), "par%d" % k, pmask)
        finish()
        return

    inc(g.sync.dma_start(w1(r), T.w1[:, :]), "ldw", 16)
    inc(g.scalar.dma_start(w2(r), T.w2[:, :]), "ldw", 16)
    inc(g.sync.dma_start(T.xs[:, :], T.x[:, :]), "ldx", 16)
    for it in SEND:
        if it in ("x0", "x1"):
            h = 0 if it == "x0" else 1
            wait(g, "ldx", 16)
            send(hcore, half(T.xs, h), half(T.xs, h), it, xmask)
        else:
            wait(g, "ldw", 32)
            dr = (r + it) % n
            send(helpers[dr] if it in HB else T.cores[dr], slot(r), slot(r), "arr%d" % r, far(core))
    order = [r] + [(r - k) % n for k in SEND if k not in ("x0", "x1") and k not in HB]
    for k in range(len(PIECES)):
        tot["par%d" % k] = pbits
    for j in order:
        if j != r:
            tot["arr%d" % j] = wbits
    nblk = len(order)

    wait(pe, "ldw", 32)
    wait(pe, "ldx", 16)
    for p, j in enumerate(order):
        if j != r:
            wait(pe, "arr%d" % j, wbits)
        for h in range(2):
            i = 2 * p + h
            k, u = i % NB, i // NB
            if u > 0:
                wait(pe, "ga_%d" % k, u)
            inc(pe.matmul(T["hp%d" % k][:, 0:HALF], w1(j), half(T.xs, h), True, True), "m1_%d" % k, 1)
        for h in range(2):
            i = 2 * p + h
            k, u = i % NB, i // NB
            wait(pe, "ga_%d" % k, u + 1)
            for s in range(2):
                q = 2 * h + s
                ins = pe.matmul(T["yp%d" % q][:, 0:QUART], w2(j),
                                T.hs[:, k * HALF + s * QUART:k * HALF + (s + 1) * QUART], p == 0, p == nblk - 1)
                inc(ins, ("yd%d" % q) if p == nblk - 1 else ("m2_%d" % k), 1)

    for i in range(2 * nblk):
        k, u = i % NB, i // NB
        wait(act, "m1_%d" % k, u + 1)
        if u > 0:
            wait(act, "m2_%d" % k, 2 * u)
        inc(act.activation(half(T.hs, k), T["hp%d" % k][:, 0:HALF], gelu), "ga_%d" % k, 1)

    for k, (a, b) in enumerate(PIECES):
        wait(g.vector, "par%d" % k, pbits)
        for q in range(a, b):
            wait(g.vector, "yd%d" % q, 1)
            inc(g.vector.tensor_tensor(quarts(T.ys, q, q + 1), T["yp%d" % q][:, 0:QUART],
                                       quarts(T.part, q, q + 1), AluOpType.add), "cq%d" % q, 1)
            wait(g.sync, "cq%d" % q, 1)
        inc(g.sync.dma_start(quarts(T.y, a, b), quarts(T.ys, a, b)), "st", 16)
    wait(g.sync, "st", 16 * len(PIECES))
    finish()
